import numpy as np
import ml_dtypes


def mxq(x, axis, fmt="e4m3"):
    dtype, down = {"e4m3": (ml_dtypes.float8_e4m3fn, 7), "e5m2": (ml_dtypes.float8_e5m2, 14)}[fmt]
    v = np.moveaxis(np.asarray(x, np.float32).astype(ml_dtypes.bfloat16).astype(np.float64), axis, -1)
    blocks = v.reshape(v.shape[:-1] + (-1, 32))
    amax = np.abs(blocks).max(-1, keepdims=True)
    byte = np.maximum(np.where(amax > 0, np.frexp(amax)[1] - 1 + 127, 0) - down, 1)
    scale = np.exp2(byte - 127.0)
    codes = (blocks / scale).astype(np.float32).astype(dtype).astype(np.float64)
    return np.moveaxis((codes * scale).reshape(v.shape), -1, axis)


WIDE = False


def mx_kscale(k):
    if not WIDE:
        return np.ones(k)
    levels = np.array([10, -10, 5, -5, 0])
    if k % 512:
        return np.exp2(np.random.permutation(np.resize(levels, k // 32))).repeat(32)
    a = np.empty((k // 512, 16))
    for p in range(k // 512):
        a[p, :8] = np.random.permutation(np.resize(levels, 8))
        for g in range(8):
            far = levels[np.abs(levels - a[p, g]) >= 10]
            a[p, g + 8] = far[np.random.randint(len(far))]
    return np.exp2(a.ravel()).repeat(32)


BF16 = ml_dtypes.bfloat16


def bf(x):
    return np.asarray(x, np.float32).astype(BF16)


def f64(x):
    return np.asarray(x).astype(np.float64)


E, R, K, N, TWO = 1024, 512, 1024, 512, 2


def draw0():
    s, t = mx_kscale(R), mx_kscale(K)
    edge = np.random.standard_normal((E, R)) * s
    wr = np.random.standard_normal((R, K)) / np.sqrt(R) / s[:, None]
    br = 0.5 * np.random.standard_normal(K)
    x = np.random.standard_normal((TWO, E, K)) * t
    wa = np.random.standard_normal((K, N)) / np.sqrt(K) / t[:, None]
    wb = np.random.standard_normal((K, N)) / np.sqrt(K) / t[:, None]
    return {"edge": bf(edge), "wr": bf(wr), "br": bf(br), "x": bf(x), "wa": bf(wa), "wb": bf(wb)}


def radial_weights(edge, wr, br):
    return (mxq(edge, 1, "e4m3") @ mxq(wr, 0, "e4m3")) + br[None, :]


def so2_mix(u, v, wa, wb):
    uq, vq = mxq(u, 1, "e4m3"), mxq(v, 1, "e4m3")
    waq, wbq = mxq(wa, 0, "e4m3"), mxq(wb, 0, "e4m3")
    out_re = (uq @ waq) - (vq @ wbq)
    out_im = (uq @ wbq) + (vq @ waq)
    return out_re, out_im


def core(edge, wr, br, x, wa, wb):
    x = f64(x)
    r = radial_weights(f64(edge), f64(wr), f64(br))
    u = x[0] * r
    v = x[1] * r
    out_re, out_im = so2_mix(u, v, f64(wa), f64(wb))
    return np.stack((out_re, out_im), axis=0)


def e4m3fn_bytes(y):
    return np.clip(np.asarray(y, np.float64), -448.0, 448.0).astype(np.float32).astype(ml_dtypes.float8_e4m3fn).view(np.uint8)


def e4m3fn_values(b):
    return np.asarray(b, np.uint8).view(ml_dtypes.float8_e4m3fn).astype(np.float64)


def setup_inputs():
    d = draw0()
    x0 = np.asarray(d['wr']).astype(np.float64)
    s = (np.max(np.abs(x0), axis=(1,), keepdims=True) / 448.0).astype(np.float32)
    out = {}
    for k, v in d.items():
        if k == 'wr':
            out['wr_bytes'] = e4m3fn_bytes(x0 / s.astype(np.float64))
            out['wr_scale'] = s
        else:
            out[k] = v
    return out


def reference(edge, wr_bytes, wr_scale, br, x, wa, wb):
    return core(edge, e4m3fn_values(wr_bytes) * wr_scale.astype(np.float64), br, x, wa, wb)

@@ -1,0 +1,318 @@
+from contextlib import ExitStack
+
+import concourse.mybir as mybir
+from concourse.masks import make_identity
+
+E, R, K, N = 1024, 512, 1024, 512
+FLOPS = 2 * E * R * K + 4 * 2 * E * K * N
+
+F32 = mybir.dt.float32
+BF16 = mybir.dt.bfloat16
+U32 = mybir.dt.uint32
+U8 = mybir.dt.uint8
+FP8 = mybir.dt.float8_e4m3fn
+FP8X4 = mybir.dt.float8_e4m3fn_x4
+ALU = mybir.AluOpType
+ACT = mybir.ActivationFunctionType
+
+P = 128
+PACK = 4
+K_PASS = P * PACK
+G = K // K_PASS
+TILES = E // P
+PAIRS = TILES // 2
+RUN = 4
+BANKS = 8
+UV_BUFS = 4
+
+
+def tile_escnso2radialconvolution_kernel(tc, edge, wr_bytes, wr_scale, br, x, wa, wb, out):
+    nc = tc.nc
+    edge_v = edge.rearrange("(p i) r -> p i r", i=TILES)
+    x_v = x.rearrange("s (p i) k -> p i s k", i=TILES)
+    out_v = out.rearrange("s (p i) n -> p i s n", i=TILES)
+    wr_v = wr_bytes.rearrange("(p j) c -> p j c", j=PACK)
+    w_v = [w.rearrange("(g p j) n -> g p j n", p=P, j=PACK) for w in (wa, wb)]
+
+    with ExitStack() as ctx:
+        sb = ctx.enter_context(tc.tile_pool(name="sb", bufs=1))
+        ps = ctx.enter_context(tc.psum_pool(name="ps", bufs=1))
+        ctx.enter_context(tc.manual_schedule())
+
+        def tiles(name, count, shape, dtype):
+            return [sb.tile(shape, dtype, name="%s%d" % (name, n), align_bytes=64) for n in range(count)]
+
+        ident = sb.tile([P, P], F32, name="ident")
+        warm = sb.tile([P, 8], F32, name="warm")
+        scale = sb.tile([P, PACK], F32, name="scale")
+        bias_bf = sb.tile([P, G, PACK], BF16, name="bias_bf")
+        bias = sb.tile([P, G, PACK], F32, name="bias")
+        wr_raw = tiles("wr_raw", 2, [P, 2, K], U8)
+        wr_wide = tiles("wr_wide", G, [P, PACK, K_PASS], BF16)
+        wr_grp = tiles("wr_grp", G, [P, K_PASS * PACK], BF16)
+        wr_codes = tiles("wr_codes", G, [P, K_PASS], U32)
+        wr_scales = tiles("wr_scales", G, [P, K_PASS], U8)
+        edge_raw = tiles("edge_raw", PAIRS, [P, 2, R], BF16)
+        edge_grp = tiles("edge_grp", PAIRS, [P, 2 * P * PACK], BF16)
+        edge_codes = tiles("edge_codes", PAIRS, [P, 2 * P], U32)
+        edge_scales = tiles("edge_scales", PAIRS, [P, 2 * P], U8)
+        x_raw = tiles("x_raw", TILES, [P, 2, K], BF16)
+        radial = tiles("radial", PAIRS * G, [P, 2, P * PACK], F32)
+        w_raw = tiles("w_raw", 2 * G, [P, PACK, N], BF16)
+        w_grp = tiles("w_grp", 2 * G, [P, N * PACK], BF16)
+        w_codes = tiles("w_codes", 2 * G, [P, N], U32)
+        w_scales = tiles("w_scales", 2 * G, [P, N], U8)
+        uv_grp = tiles("uv_grp", UV_BUFS, [P, 2 * P * PACK], BF16)
+        uv_codes = tiles("uv_codes", TILES * G, [P, 2 * P], U32)
+        uv_scales = tiles("uv_scales", TILES * G, [P, 2 * P], U8)
+        u_wa = tiles("u_wa", 2, [P, N], F32)
+        res_re = tiles("res_re", TILES, [P, N], F32)
+        res_im = tiles("res_im", TILES, [P, N], F32)
+
+        banks = [ps.tile([P, N], F32, name="bank%d" % n) for n in range(BANKS)]
+        free = list(range(BANKS))
+        held = {}
+
+        def take_bank(key):
+            held[key] = free[0]
+            free.remove(held[key])
+            return banks[held[key]]
+
+        def last_read(key):
+            free.append(held[key])
+            return banks[held[key]]
+
+        def quantize(codes, scales, grouped):
+            nc.vector.quantize_mx(out=codes[:].bitcast(FP8X4), scales=scales[:], in_=grouped[:])
+
+        def widen(g, j, on_vector):
+            src = wr_raw[j // 2][:, j % 2, g * K_PASS:(g + 1) * K_PASS].bitcast(FP8)
+            if on_vector:
+                nc.vector.tensor_scalar(out=wr_wide[g][:, j, :], in0=src, scalar1=scale[:, j:j + 1], scalar2=None, op0=ALU.mult)
+            else:
+                nc.scalar.activation(out=wr_wide[g][:, j, :], in_=src, func=ACT.Copy, scale=scale[:, j:j + 1])
+
+        def group_wr(g, on_vector):
+            dst = wr_grp[g][:].rearrange("p (t m j) -> p m t j", t=PACK, j=PACK)
+            src = wr_wide[g][:].rearrange("p j (m t) -> p m t j", t=PACK)
+            if on_vector:
+                nc.vector.tensor_copy(out=dst, in_=src)
+            else:
+                nc.scalar.copy(out=dst, in_=src)
+
+        def group_w(w, g, on_vector):
+            dst = w_grp[2 * g + w][:].rearrange("p (c q j) -> p c j q", q=RUN, j=PACK)
+            src = w_raw[2 * g + w][:].rearrange("p j (c q) -> p c j q", q=RUN)
+            if on_vector:
+                nc.vector.tensor_copy(out=dst, in_=src)
+            else:
+                nc.scalar.copy(out=dst, in_=src)
+
+        def quantize_w(w, g):
+            quantize(w_codes[2 * g + w], w_scales[2 * g + w], w_grp[2 * g + w])
+
+        def turn_edge(pair):
+            bank = take_bank(("edge", pair))[:].rearrange("p (i h e) -> p i h e", i=2, h=2)
+            for i in range(2):
+                words = edge_raw[pair][:, i, :].bitcast(F32)
+                for h in range(2):
+                    nc.tensor.transpose(bank[:, i, h, :], words[:, h::2], ident[:])
+
+        def empty_edge(pair):
+            nc.scalar.copy(
+                out=edge_grp[pair][:].bitcast(F32).rearrange("p (i e h) -> p i e h", i=2, h=2),
+                in_=last_read(("edge", pair))[:].rearrange("p (i h e) -> p i e h", i=2, h=2))
+
+        def radial_passes(pair, g, half):
+            bank = take_bank(("radial", pair, g, half))
+            for n in range(2):
+                cols = slice((2 * half + n) * P, (2 * half + n + 1) * P)
+                nc.tensor.matmul_mx(
+                    out=bank[:, n * 2 * P:(n + 1) * 2 * P],
+                    lhsT=wr_codes[g][:, cols].bitcast(FP8X4), lhsT_scale=wr_scales[g][:, cols],
+                    rhs=edge_codes[pair][:].bitcast(FP8X4), rhs_scale=edge_scales[pair][:],
+                    start=True, stop=True)
+
+        def empty_radial(pair, g, half):
+            bank = last_read(("radial", pair, g, half))
+            dst = radial[G * pair + g][:].rearrange("p i (c t q) -> p t i c q", t=PACK, q=RUN)
+            for n in range(2):
+                t = 2 * half + n
+                nc.scalar.activation(
+                    out=dst[:, t], in_=bank[:, n * 2 * P:(n + 1) * 2 * P].rearrange("p (i c q) -> p i c q", i=2, q=RUN),
+                    func=ACT.Identity, bias=bias[:, g, t:t + 1])
+
+        def turn_x(i, g):
+            bank = take_bank(("x", i, g))[:].rearrange("p (s c h q) -> p s h c q", s=2, h=2, q=RUN)
+            for s in range(2):
+                words = x_raw[i][:, s, g * K_PASS:(g + 1) * K_PASS].bitcast(F32)
+                for h in range(2):
+                    nc.tensor.transpose(bank[:, s, h], words[:, h::2], ident[:])
+
+        def modulate(i, g):
+            turned = last_read(("x", i, g))[:].bitcast(BF16).rearrange("p (s c h q j) -> p s c h j q", s=2, h=2, q=RUN, j=2)
+            r = radial[G * (i // 2) + g][:, i % 2, :].rearrange("p (c h j q) -> p c h j q", h=2, j=2, q=RUN)
+            nc.vector.tensor_tensor(
+                out=uv_grp[(G * i + g) % UV_BUFS][:].rearrange("p (s c q h j) -> p s c h j q", s=2, q=RUN, h=2, j=2),
+                in0=turned, in1=r.unsqueeze(1).to_broadcast([P, 2, P // RUN, 2, 2, RUN]), op=ALU.mult)
+
+        def quantize_uv(i, g):
+            quantize(uv_codes[G * i + g], uv_scales[G * i + g], uv_grp[(G * i + g) % UV_BUFS])
+
+        def product(name, i, g, terms):
+            acc = take_bank((name, i)) if g == 0 else banks[held[(name, i)]]
+            for n, (s, w) in enumerate(terms):
+                cols = slice(s * P, (s + 1) * P)
+                nc.tensor.matmul_mx(
+                    out=acc[:], lhsT=uv_codes[G * i + g][:, cols].bitcast(FP8X4), lhsT_scale=uv_scales[G * i + g][:, cols],
+                    rhs=w_codes[2 * g + w][:].bitcast(FP8X4), rhs_scale=w_scales[2 * g + w][:],
+                    start=(g == 0 and n == 0), stop=(g == G - 1 and n == len(terms) - 1))
+
+        def mix_uwa(i, g):
+            product("uwa", i, g, [(0, 0)])
+
+        def mix_vwb(i, g):
+            product("vwb", i, g, [(1, 1)])
+
+        def mix_im(i, g):
+            product("im", i, g, [(0, 1), (1, 0)])
+
+        def empty_uwa(i):
+            nc.scalar.copy(out=u_wa[i % 2][:], in_=last_read(("uwa", i))[:])
+
+        def finish_re(i):
+            nc.vector.tensor_tensor(out=res_re[i][:], in0=u_wa[i % 2][:], in1=last_read(("vwb", i))[:], op=ALU.subtract)
+            nc.sync.dma_start(out=out_v[:, i, 0, :], in_=res_re[i][:])
+
+        def finish_im(i):
+            nc.scalar.copy(out=res_im[i][:], in_=last_read(("im", i))[:])
+            nc.sync.dma_start(out=out_v[:, i, 1, :], in_=res_im[i][:])
+
+        def radial_half(pair, g, half):
+            radial_passes(pair, g, half)
+            empty_radial(pair, g, half)
+
+        def quantize_edge(pair):
+            quantize(edge_codes[pair], edge_scales[pair], edge_grp[pair])
+
+        def quantize_wr(g):
+            quantize(wr_codes[g], wr_scales[g], wr_grp[g])
+
+        def load_edge(pair):
+            nc.sync.dma_start(out=edge_raw[pair][:], in_=edge_v[:, 2 * pair:2 * pair + 2, :])
+
+        def load_x(i):
+            nc.sync.dma_start(out=x_raw[i][:], in_=x_v[:, i])
+
+        def load_w(w, g):
+            nc.sync.dma_start(out=w_raw[2 * g + w][:], in_=w_v[w][g])
+
+        nc.scalar.dma_start(out=scale[:], in_=wr_scale.rearrange("(p j) o -> p (j o)", j=PACK))
+        nc.sync.dma_start(out=wr_raw[0][:], in_=wr_v[:, 0:2, :])
+        nc.sync.dma_start(out=wr_raw[1][:], in_=wr_v[:, 2:4, :])
+        load_edge(0)
+        nc.scalar.dma_start(out=bias_bf[:], in_=br.rearrange("(g p t) -> p g t", p=P, t=PACK))
+        load_edge(1)
+        load_x(0)
+        load_w(0, 0)
+        load_w(1, 0)
+        load_x(1)
+        load_w(0, 1)
+        load_edge(2)
+        load_w(1, 1)
+        load_x(2)
+        load_edge(3)
+        for i in range(3, TILES):
+            load_x(i)
+
+        nc.vector.memset(warm[:], 0.0)
+        nc.scalar.activation(out=warm[:], in_=warm[:], func=ACT.Identity)
+        make_identity(nc, ident[:])
+
+        for j in range(PACK):
+            widen(0, j, True)
+        for j in range(PACK):
+            widen(1, j, j == 0)
+        turn_edge(0)
+        empty_edge(0)
+        turn_edge(1)
+        group_wr(0, True)
+        group_wr(1, False)
+        empty_edge(1)
+        nc.vector.tensor_copy(out=bias[:], in_=bias_bf[:])
+        quantize_edge(0)
+        quantize_wr(0)
+        turn_x(0, 0)
+        turn_x(0, 1)
+        radial_half(0, 0, 0)
+        radial_half(0, 0, 1)
+        group_w(0, 0, True)
+        quantize_wr(1)
+        radial_half(0, 1, 0)
+        radial_half(0, 1, 1)
+        quantize_edge(1)
+        quantize_w(0, 0)
+        group_w(1, 0, True)
+        turn_x(1, 0)
+        turn_x(1, 1)
+        group_w(0, 1, False)
+        modulate(0, 0)
+        turn_edge(2)
+        modulate(0, 1)
+        radial_half(1, 0, 0)
+        radial_half(1, 0, 1)
+        group_w(1, 1, False)
+        quantize_uv(0, 0)
+        quantize_w(1, 0)
+        quantize_uv(0, 1)
+        modulate(1, 0)
+        quantize_w(0, 1)
+        turn_x(2, 0)
+        empty_edge(2)
+        mix_uwa(0, 0)
+        mix_im(0, 0)
+        radial_half(1, 1, 0)
+        mix_uwa(0, 1)
+        radial_half(1, 1, 1)
+        modulate(1, 1)
+        quantize_uv(1, 0)
+        quantize_w(1, 1)
+        quantize_edge(2)
+        empty_uwa(0)
+        turn_x(2, 1)
+        turn_edge(3)
+        empty_edge(3)
+        mix_im(0, 1)
+        finish_im(0)
+        mix_vwb(0, 0)
+        mix_vwb(0, 1)
+
+        for i in range(2, TILES + 1):
+            m = i - 1
+            unit = i + 2
+            if i < TILES:
+                modulate(i, 0)
+            quantize_uv(m, 1)
+            if i == 2:
+                quantize_edge(3)
+            finish_re(m - 1)
+            mix_uwa(m, 0)
+            mix_im(m, 0)
+            if unit < PAIRS * G:
+                radial_half(unit // G, unit % G, 0)
+            if i + 1 < TILES:
+                turn_x(i + 1, 0)
+            if i < TILES:
+                modulate(i, 1)
+                quantize_uv(i, 0)
+            if i + 1 < TILES:
+                turn_x(i + 1, 1)
+            mix_uwa(m, 1)
+            empty_uwa(m)
+            mix_vwb(m, 0)
+            mix_vwb(m, 1)
+            mix_im(m, 1)
+            finish_im(m)
+            if unit < PAIRS * G:
+                radial_half(unit // G, unit % G, 1)
+        finish_re(TILES - 1)

@@ -24,6 +24,9 @@ PAIRS = TILES // 2
 RUN = 4
 BANKS = 8
 UV_BUFS = 4
+SPLIT_FROM = 4
+HALVES = 16
+HALF0 = 5
 
 
 def tile_escnso2radialconvolution_kernel(tc, edge, wr_bytes, wr_scale, br, x, wa, wb, out):
@@ -57,6 +60,7 @@ def tile_escnso2radialconvolution_kernel(tc, edge, wr_bytes, wr_scale, br, x, wa
         edge_codes = tiles("edge_codes", PAIRS, [P, 2 * P], U32)
         edge_scales = tiles("edge_scales", PAIRS, [P, 2 * P], U8)
         x_raw = tiles("x_raw", TILES, [P, 2, K], BF16)
+        x_split = tiles("x_split", 2, [P, 2 * G, 2, P], F32)
         radial = tiles("radial", PAIRS * G, [P, 2, P * PACK], F32)
         w_raw = tiles("w_raw", 2 * G, [P, PACK, N], BF16)
         w_grp = tiles("w_grp", 2 * G, [P, N * PACK], BF16)
@@ -147,7 +151,14 @@ def tile_escnso2radialconvolution_kernel(tc, edge, wr_bytes, wr_scale, br, x, wa
             for s in range(2):
                 words = x_raw[i][:, s, g * K_PASS:(g + 1) * K_PASS].bitcast(F32)
                 for h in range(2):
-                    nc.tensor.transpose(bank[:, s, h], words[:, h::2], ident[:])
+                    if i >= SPLIT_FROM:
+                        nc.tensor.transpose(bank[:, s, h], x_split[i % 2][:, s * G + g, h, :], ident[:])
+                    else:
+                        nc.tensor.transpose(bank[:, s, h], words[:, h::2], ident[:])
+
+        def split_x(i):
+            words = x_raw[i][:].rearrange("p s k -> p (s k)").bitcast(F32)
+            nc.scalar.copy(out=x_split[i % 2][:], in_=words.rearrange("p (a w h) -> p a h w", h=2, w=P))
 
         def modulate(i, g):
             turned = last_read(("x", i, g))[:].bitcast(BF16).rearrange("p (s c h q j) -> p s c h j q", s=2, h=2, q=RUN, j=2)
@@ -232,7 +243,7 @@ def tile_escnso2radialconvolution_kernel(tc, edge, wr_bytes, wr_scale, br, x, wa
         for j in range(PACK):
             widen(0, j, True)
         for j in range(PACK):
-            widen(1, j, j == 0)
+            widen(1, j, False)
         turn_edge(0)
         empty_edge(0)
         turn_edge(1)
@@ -240,8 +251,8 @@ def tile_escnso2radialconvolution_kernel(tc, edge, wr_bytes, wr_scale, br, x, wa
         group_wr(1, False)
         empty_edge(1)
         nc.vector.tensor_copy(out=bias[:], in_=bias_bf[:])
-        quantize_edge(0)
         quantize_wr(0)
+        quantize_edge(0)
         turn_x(0, 0)
         turn_x(0, 1)
         radial_half(0, 0, 0)
@@ -256,63 +267,80 @@ def tile_escnso2radialconvolution_kernel(tc, edge, wr_bytes, wr_scale, br, x, wa
         turn_x(1, 0)
         turn_x(1, 1)
         group_w(0, 1, False)
-        modulate(0, 0)
-        turn_edge(2)
-        modulate(0, 1)
-        radial_half(1, 0, 0)
-        radial_half(1, 0, 1)
         group_w(1, 1, False)
-        quantize_uv(0, 0)
+        radial_passes(1, 0, 0)
+        radial_passes(1, 0, 1)
+        turn_edge(2)
+        modulate(0, 0)
         quantize_w(1, 0)
-        quantize_uv(0, 1)
-        modulate(1, 0)
-        quantize_w(0, 1)
+        quantize_uv(0, 0)
         turn_x(2, 0)
-        empty_edge(2)
-        mix_uwa(0, 0)
         mix_im(0, 0)
-        radial_half(1, 1, 0)
+        modulate(0, 1)
+        mix_uwa(0, 0)
+        quantize_w(0, 1)
+        quantize_uv(0, 1)
         mix_uwa(0, 1)
-        radial_half(1, 1, 1)
-        modulate(1, 1)
-        quantize_uv(1, 0)
-        quantize_w(1, 1)
-        quantize_edge(2)
-        empty_uwa(0)
+        modulate(1, 0)
+        empty_edge(2)
+        empty_radial(1, 0, 0)
+        empty_radial(1, 0, 1)
         turn_x(2, 1)
-        turn_edge(3)
-        empty_edge(3)
+        quantize_w(1, 1)
+        quantize_uv(1, 0)
+        quantize_edge(2)
+        radial_half(1, 1, 0)
         mix_im(0, 1)
-        finish_im(0)
+        radial_half(1, 1, 1)
         mix_vwb(0, 0)
         mix_vwb(0, 1)
+        radial_passes(2, 0, 0)
+        empty_uwa(0)
+        turn_edge(3)
+        modulate(1, 1)
+        finish_im(0)
+        empty_radial(2, 0, 0)
+        empty_edge(3)
 
         for i in range(2, TILES + 1):
             m = i - 1
-            unit = i + 2
-            if i < TILES:
+            last = i == TILES
+            early, late = 2 * i + HALF0, 2 * i + HALF0 + 1
+            if not last:
                 modulate(i, 0)
             quantize_uv(m, 1)
-            if i == 2:
+            if not last:
+                quantize_uv(i, 0)
+            if i == 3:
                 quantize_edge(3)
-            finish_re(m - 1)
-            mix_uwa(m, 0)
+            mix_vwb(m, 0)
             mix_im(m, 0)
-            if unit < PAIRS * G:
-                radial_half(unit // G, unit % G, 0)
+            mix_uwa(m, 0)
+            if SPLIT_FROM <= i + 2 < TILES:
+                split_x(i + 2)
             if i + 1 < TILES:
                 turn_x(i + 1, 0)
-            if i < TILES:
-                modulate(i, 1)
-                quantize_uv(i, 0)
-            if i + 1 < TILES:
                 turn_x(i + 1, 1)
-            mix_uwa(m, 1)
-            empty_uwa(m)
-            mix_vwb(m, 0)
-            mix_vwb(m, 1)
-            mix_im(m, 1)
-            finish_im(m)
-            if unit < PAIRS * G:
-                radial_half(unit // G, unit % G, 1)
+            if early < HALVES:
+                radial_passes(early // 4, early // 2 % 2, early % 2)
+            if not last:
+                modulate(i, 1)
+            if early < HALVES:
+                empty_radial(early // 4, early // 2 % 2, early % 2)
+            if last:
+                mix_uwa(m, 1)
+                mix_vwb(m, 1)
+                mix_im(m, 1)
+                finish_re(m - 1)
+                empty_uwa(m)
+                finish_im(m)
+            else:
+                mix_im(m, 1)
+                mix_uwa(m, 1)
+                mix_vwb(m, 1)
+                finish_re(m - 1)
+                finish_im(m)
+                empty_uwa(m)
+            if late < HALVES:
+                radial_half(late // 4, late // 2 % 2, late % 2)
         finish_re(TILES - 1)

@@ -23,7 +23,9 @@ TILES = E // P
 PAIRS = TILES // 2
 RUN = 4
 BANKS = 8
-UV_BUFS = 4
+UV_BUFS = 3
+ON_GPSIMD = (3, 4)
+UWA_BUFS = 3
 SPLIT_FROM = 4
 HALVES = 16
 HALF0 = 5
@@ -49,29 +51,30 @@ def tile_escnso2radialconvolution_kernel(tc, edge, wr_bytes, wr_scale, br, x, wa
         warm = sb.tile([P, 8], F32, name="warm")
         scale = sb.tile([P, PACK], F32, name="scale")
         bias_bf = sb.tile([P, G, PACK], BF16, name="bias_bf")
-        bias = sb.tile([P, G, PACK], F32, name="bias")
         wr_raw = tiles("wr_raw", 2, [P, 2, K], U8)
         wr_wide = tiles("wr_wide", G, [P, PACK, K_PASS], BF16)
         wr_grp = tiles("wr_grp", G, [P, K_PASS * PACK], BF16)
         wr_codes = tiles("wr_codes", G, [P, K_PASS], U32)
         wr_scales = tiles("wr_scales", G, [P, K_PASS], U8)
         edge_raw = tiles("edge_raw", PAIRS, [P, 2, R], BF16)
-        edge_grp = tiles("edge_grp", PAIRS, [P, 2 * P * PACK], BF16)
-        edge_codes = tiles("edge_codes", PAIRS, [P, 2 * P], U32)
-        edge_scales = tiles("edge_scales", PAIRS, [P, 2 * P], U8)
+        edge_grp = tiles("edge_grp", PAIRS // 2, [P, 4 * P * PACK], BF16)
+        edge_codes = tiles("edge_codes", PAIRS // 2, [P, 4 * P], U32)
+        edge_scales = tiles("edge_scales", PAIRS // 2, [P, 4 * P], U8)
         x_raw = tiles("x_raw", TILES, [P, 2, K], BF16)
         x_split = tiles("x_split", 2, [P, 2 * G, 2, P], F32)
         radial = tiles("radial", PAIRS * G, [P, 2, P * PACK], F32)
         w_raw = tiles("w_raw", 2 * G, [P, PACK, N], BF16)
         w_grp = tiles("w_grp", 2 * G, [P, N * PACK], BF16)
+        w_grp[1] = w_grp[0]
         w_codes = tiles("w_codes", 2 * G, [P, N], U32)
         w_scales = tiles("w_scales", 2 * G, [P, N], U8)
-        uv_grp = tiles("uv_grp", UV_BUFS, [P, 2 * P * PACK], BF16)
-        uv_codes = tiles("uv_codes", TILES * G, [P, 2 * P], U32)
-        uv_scales = tiles("uv_scales", TILES * G, [P, 2 * P], U8)
-        u_wa = tiles("u_wa", 2, [P, N], F32)
+        uv_grp = tiles("uv_grp", UV_BUFS, [P, 4 * P * PACK], BF16)
+        uv_codes = tiles("uv_codes", TILES + 1, [P, 4 * P], U32)
+        uv_scales = tiles("uv_scales", TILES + 1, [P, 4 * P], U8)
+        u_wa = tiles("u_wa", UWA_BUFS, [P, N], F32)
+        v_wb = tiles("v_wb", 2, [P, N], F32)
         res_re = tiles("res_re", TILES, [P, N], F32)
-        res_im = tiles("res_im", TILES, [P, N], F32)
+        res_im = tiles("res_im", 4, [P, N], F32)
 
         banks = [ps.tile([P, N], F32, name="bank%d" % n) for n in range(BANKS)]
         free = list(range(BANKS))
@@ -86,8 +89,9 @@ def tile_escnso2radialconvolution_kernel(tc, edge, wr_bytes, wr_scale, br, x, wa
             free.append(held[key])
             return banks[held[key]]
 
-        def quantize(codes, scales, grouped):
-            nc.vector.quantize_mx(out=codes[:].bitcast(FP8X4), scales=scales[:], in_=grouped[:])
+        def quantize(codes, scales, grouped, first, count):
+            nc.vector.quantize_mx(out=codes[:, first:first + count].bitcast(FP8X4), scales=scales[:, first:first + count],
+                                  in_=grouped[:, PACK * first:PACK * (first + count)])
 
         def widen(g, j, on_vector):
             src = wr_raw[j // 2][:, j % 2, g * K_PASS:(g + 1) * K_PASS].bitcast(FP8)
@@ -112,8 +116,13 @@ def tile_escnso2radialconvolution_kernel(tc, edge, wr_bytes, wr_scale, br, x, wa
             else:
                 nc.scalar.copy(out=dst, in_=src)
 
+        def group_w_gpsimd(w, g):
+            nc.gpsimd.tensor_scalar(
+                out=w_grp[2 * g + w][:].rearrange("p (n j) -> p n j", j=PACK), in0=w_raw[2 * g + w][:].rearrange("p j n -> p n j"),
+                scalar1=1.0, scalar2=0.0, op0=ALU.mult, op1=ALU.add)
+
         def quantize_w(w, g):
-            quantize(w_codes[2 * g + w], w_scales[2 * g + w], w_grp[2 * g + w])
+            quantize(w_codes[2 * g + w], w_scales[2 * g + w], w_grp[2 * g + w], 0, N)
 
         def turn_edge(pair):
             bank = take_bank(("edge", pair))[:].rearrange("p (i h e) -> p i h e", i=2, h=2)
@@ -124,17 +133,18 @@ def tile_escnso2radialconvolution_kernel(tc, edge, wr_bytes, wr_scale, br, x, wa
 
         def empty_edge(pair):
             nc.scalar.copy(
-                out=edge_grp[pair][:].bitcast(F32).rearrange("p (i e h) -> p i e h", i=2, h=2),
+                out=edge_grp[pair // 2][:, pair % 2 * 2 * K_PASS:(pair % 2 + 1) * 2 * K_PASS].bitcast(F32).rearrange("p (i e h) -> p i e h", i=2, h=2),
                 in_=last_read(("edge", pair))[:].rearrange("p (i h e) -> p i e h", i=2, h=2))
 
         def radial_passes(pair, g, half):
             bank = take_bank(("radial", pair, g, half))
+            edges = slice(pair % 2 * 2 * P, (pair % 2 + 1) * 2 * P)
             for n in range(2):
                 cols = slice((2 * half + n) * P, (2 * half + n + 1) * P)
                 nc.tensor.matmul_mx(
                     out=bank[:, n * 2 * P:(n + 1) * 2 * P],
                     lhsT=wr_codes[g][:, cols].bitcast(FP8X4), lhsT_scale=wr_scales[g][:, cols],
-                    rhs=edge_codes[pair][:].bitcast(FP8X4), rhs_scale=edge_scales[pair][:],
+                    rhs=edge_codes[pair // 2][:, edges].bitcast(FP8X4), rhs_scale=edge_scales[pair // 2][:, edges],
                     start=True, stop=True)
 
         def empty_radial(pair, g, half):
@@ -144,7 +154,7 @@ def tile_escnso2radialconvolution_kernel(tc, edge, wr_bytes, wr_scale, br, x, wa
                 t = 2 * half + n
                 nc.scalar.activation(
                     out=dst[:, t], in_=bank[:, n * 2 * P:(n + 1) * 2 * P].rearrange("p (i c q) -> p i c q", i=2, q=RUN),
-                    func=ACT.Identity, bias=bias[:, g, t:t + 1])
+                    func=ACT.Identity, bias=bias_bf[:, g, t:t + 1])
 
         def turn_x(i, g):
             bank = take_bank(("x", i, g))[:].rearrange("p (s c h q) -> p s h c q", s=2, h=2, q=RUN)
@@ -160,54 +170,65 @@ def tile_escnso2radialconvolution_kernel(tc, edge, wr_bytes, wr_scale, br, x, wa
             words = x_raw[i][:].rearrange("p s k -> p (s k)").bitcast(F32)
             nc.scalar.copy(out=x_split[i % 2][:], in_=words.rearrange("p (a w h) -> p a h w", h=2, w=P))
 
-        def modulate(i, g):
-            turned = last_read(("x", i, g))[:].bitcast(BF16).rearrange("p (s c h q j) -> p s c h j q", s=2, h=2, q=RUN, j=2)
+        def modulate(i, g, parts=(0, 1)):
+            count = len(parts)
+            bank = last_read(("x", i, g)) if parts[-1] == 1 else banks[held[("x", i, g)]]
+            turned = bank[:].bitcast(BF16).rearrange("p (s c h q j) -> p s c h j q", s=2, h=2, q=RUN, j=2)
             r = radial[G * (i // 2) + g][:, i % 2, :].rearrange("p (c h j q) -> p c h j q", h=2, j=2, q=RUN)
+            dst = uv_grp[(i + g) % UV_BUFS][:].rearrange("p (a s c q h j) -> p a s c h j q", a=2, s=2, q=RUN, h=2, j=2)
             nc.vector.tensor_tensor(
-                out=uv_grp[(G * i + g) % UV_BUFS][:].rearrange("p (s c q h j) -> p s c h j q", s=2, q=RUN, h=2, j=2),
-                in0=turned, in1=r.unsqueeze(1).to_broadcast([P, 2, P // RUN, 2, 2, RUN]), op=ALU.mult)
+                out=dst[:, 1 - g, parts[0]:parts[0] + count], in0=turned[:, parts[0]:parts[0] + count],
+                in1=r.unsqueeze(1).to_broadcast([P, count, P // RUN, 2, 2, RUN]), op=ALU.mult)
 
-        def quantize_uv(i, g):
-            quantize(uv_codes[G * i + g], uv_scales[G * i + g], uv_grp[(G * i + g) % UV_BUFS])
+        def quantize_uv(n, first, count):
+            quantize(uv_codes[n], uv_scales[n], uv_grp[n % UV_BUFS], first * P, count * P)
 
-        def product(name, i, g, terms):
-            acc = take_bank((name, i)) if g == 0 else banks[held[(name, i)]]
+        def product(name, i, g, terms, start, stop):
+            acc = banks[held[(name, i)]] if (name, i) in held else take_bank((name, i))
             for n, (s, w) in enumerate(terms):
-                cols = slice(s * P, (s + 1) * P)
+                cols = slice((2 * (1 - g) + s) * P, (2 * (1 - g) + s + 1) * P)
                 nc.tensor.matmul_mx(
-                    out=acc[:], lhsT=uv_codes[G * i + g][:, cols].bitcast(FP8X4), lhsT_scale=uv_scales[G * i + g][:, cols],
+                    out=acc[:], lhsT=uv_codes[i + g][:, cols].bitcast(FP8X4), lhsT_scale=uv_scales[i + g][:, cols],
                     rhs=w_codes[2 * g + w][:].bitcast(FP8X4), rhs_scale=w_scales[2 * g + w][:],
-                    start=(g == 0 and n == 0), stop=(g == G - 1 and n == len(terms) - 1))
+                    start=(start and n == 0), stop=(stop and n == len(terms) - 1))
 
         def mix_uwa(i, g):
-            product("uwa", i, g, [(0, 0)])
+            product("uwa", i, g, [(0, 0)], g == 0, g == 1)
 
         def mix_vwb(i, g):
-            product("vwb", i, g, [(1, 1)])
+            product("vwb", i, g, [(1, 1)], g == 0, g == 1)
 
         def mix_im(i, g):
-            product("im", i, g, [(0, 1), (1, 0)])
+            product("im", i, g, [(0, 1), (1, 0)], g == 0, g == 1)
 
         def empty_uwa(i):
-            nc.scalar.copy(out=u_wa[i % 2][:], in_=last_read(("uwa", i))[:])
+            nc.scalar.copy(out=u_wa[i % UWA_BUFS][:], in_=last_read(("uwa", i))[:])
 
         def finish_re(i):
-            nc.vector.tensor_tensor(out=res_re[i][:], in0=u_wa[i % 2][:], in1=last_read(("vwb", i))[:], op=ALU.subtract)
+            nc.vector.tensor_tensor(out=res_re[i][:], in0=u_wa[i % UWA_BUFS][:], in1=last_read(("vwb", i))[:], op=ALU.subtract)
             nc.sync.dma_start(out=out_v[:, i, 0, :], in_=res_re[i][:])
 
+        def empty_vwb(i):
+            nc.scalar.copy(out=v_wb[i % 2][:], in_=last_read(("vwb", i))[:])
+
+        def finish_re_gpsimd(i):
+            res = uv_grp[(i + 2) % UV_BUFS][:, 2 * K_PASS:].bitcast(F32)
+            nc.gpsimd.tensor_tensor(out=res, in0=u_wa[i % UWA_BUFS][:], in1=v_wb[i % 2][:], op=ALU.subtract)
+            nc.sync.dma_start(out=out_v[:, i, 0, :], in_=res)
+
         def finish_im(i):
-            nc.scalar.copy(out=res_im[i][:], in_=last_read(("im", i))[:])
-            nc.sync.dma_start(out=out_v[:, i, 1, :], in_=res_im[i][:])
+            nc.scalar.copy(out=res_im[i % 4][:], in_=last_read(("im", i))[:])
+            nc.sync.dma_start(out=out_v[:, i, 1, :], in_=res_im[i % 4][:])
 
         def radial_half(pair, g, half):
             radial_passes(pair, g, half)
             empty_radial(pair, g, half)
 
-        def quantize_edge(pair):
-            quantize(edge_codes[pair], edge_scales[pair], edge_grp[pair])
+        def quantize_edge(pair, pairs):
+            quantize(edge_codes[pair // 2], edge_scales[pair // 2], edge_grp[pair // 2], pair % 2 * 2 * P, pairs * 2 * P)
 
         def quantize_wr(g):
-            quantize(wr_codes[g], wr_scales[g], wr_grp[g])
+            quantize(wr_codes[g], wr_scales[g], wr_grp[g], 0, K_PASS)
 
         def load_edge(pair):
             nc.sync.dma_start(out=edge_raw[pair][:], in_=edge_v[:, 2 * pair:2 * pair + 2, :])
@@ -223,9 +244,9 @@ def tile_escnso2radialconvolution_kernel(tc, edge, wr_bytes, wr_scale, br, x, wa
         nc.sync.dma_start(out=wr_raw[1][:], in_=wr_v[:, 2:4, :])
         load_edge(0)
         nc.scalar.dma_start(out=bias_bf[:], in_=br.rearrange("(g p t) -> p g t", p=P, t=PACK))
-        load_edge(1)
-        load_x(0)
         load_w(0, 0)
+        load_x(0)
+        load_edge(1)
         load_w(1, 0)
         load_x(1)
         load_w(0, 1)
@@ -243,76 +264,73 @@ def tile_escnso2radialconvolution_kernel(tc, edge, wr_bytes, wr_scale, br, x, wa
         for j in range(PACK):
             widen(0, j, True)
         for j in range(PACK):
-            widen(1, j, False)
+            widen(1, j, j == 0)
         turn_edge(0)
         empty_edge(0)
-        turn_edge(1)
         group_wr(0, True)
         group_wr(1, False)
-        empty_edge(1)
-        nc.vector.tensor_copy(out=bias[:], in_=bias_bf[:])
+        quantize_edge(0, 1)
         quantize_wr(0)
-        quantize_edge(0)
         turn_x(0, 0)
+        radial_passes(0, 0, 0)
+        radial_passes(0, 0, 1)
+        turn_edge(1)
+        empty_radial(0, 0, 0)
+        empty_radial(0, 0, 1)
+        empty_edge(1)
         turn_x(0, 1)
-        radial_half(0, 0, 0)
-        radial_half(0, 0, 1)
         group_w(0, 0, True)
         quantize_wr(1)
+        quantize_w(0, 0)
+        group_w_gpsimd(1, 0)
         radial_half(0, 1, 0)
         radial_half(0, 1, 1)
-        quantize_edge(1)
-        quantize_w(0, 0)
-        group_w(1, 0, True)
         turn_x(1, 0)
         turn_x(1, 1)
         group_w(0, 1, False)
         group_w(1, 1, False)
+        modulate(0, 0)
+        turn_edge(2)
+        modulate(1, 0)
+        turn_x(2, 0)
+        modulate(0, 1)
+        turn_x(2, 1)
+        quantize_edge(1, 1)
+        quantize_uv(0, 2, 2)
+        quantize_w(1, 0)
         radial_passes(1, 0, 0)
         radial_passes(1, 0, 1)
-        turn_edge(2)
-        modulate(0, 0)
-        quantize_w(1, 0)
-        quantize_uv(0, 0)
-        turn_x(2, 0)
-        mix_im(0, 0)
-        modulate(0, 1)
-        mix_uwa(0, 0)
         quantize_w(0, 1)
-        quantize_uv(0, 1)
-        mix_uwa(0, 1)
-        modulate(1, 0)
+        quantize_uv(1, 0, 4)
+        mix_im(0, 0)
+        mix_uwa(0, 0)
+        modulate(1, 1)
         empty_edge(2)
         empty_radial(1, 0, 0)
         empty_radial(1, 0, 1)
-        turn_x(2, 1)
+        mix_uwa(0, 1)
         quantize_w(1, 1)
-        quantize_uv(1, 0)
-        quantize_edge(2)
+        quantize_edge(2, 1)
         radial_half(1, 1, 0)
-        mix_im(0, 1)
         radial_half(1, 1, 1)
+        mix_im(0, 1)
         mix_vwb(0, 0)
         mix_vwb(0, 1)
         radial_passes(2, 0, 0)
         empty_uwa(0)
         turn_edge(3)
-        modulate(1, 1)
         finish_im(0)
         empty_radial(2, 0, 0)
         empty_edge(3)
 
-        for i in range(2, TILES + 1):
+        for i in range(2, TILES):
             m = i - 1
-            last = i == TILES
             early, late = 2 * i + HALF0, 2 * i + HALF0 + 1
-            if not last:
-                modulate(i, 0)
-            quantize_uv(m, 1)
-            if not last:
-                quantize_uv(i, 0)
+            modulate(i, 0)
+            quantize_uv(i, 0, 2)
             if i == 3:
-                quantize_edge(3)
+                quantize_edge(3, 1)
+            quantize_uv(i, 2, 2)
             mix_vwb(m, 0)
             mix_im(m, 0)
             mix_uwa(m, 0)
@@ -323,24 +341,44 @@ def tile_escnso2radialconvolution_kernel(tc, edge, wr_bytes, wr_scale, br, x, wa
                 turn_x(i + 1, 1)
             if early < HALVES:
                 radial_passes(early // 4, early // 2 % 2, early % 2)
-            if not last:
-                modulate(i, 1)
+            modulate(i, 1, (0, 1) if i + 1 < TILES else (0,))
             if early < HALVES:
                 empty_radial(early // 4, early // 2 % 2, early % 2)
-            if last:
+            if m in ON_GPSIMD:
                 mix_uwa(m, 1)
                 mix_vwb(m, 1)
                 mix_im(m, 1)
-                finish_re(m - 1)
-                empty_uwa(m)
-                finish_im(m)
             else:
                 mix_im(m, 1)
                 mix_uwa(m, 1)
                 mix_vwb(m, 1)
+            if m - 1 in ON_GPSIMD:
+                finish_re_gpsimd(m - 1)
+            elif i + 1 < TILES:
                 finish_re(m - 1)
+            if m in ON_GPSIMD:
+                empty_uwa(m)
+                empty_vwb(m)
+                finish_im(m)
+            else:
                 finish_im(m)
                 empty_uwa(m)
             if late < HALVES:
                 radial_half(late // 4, late // 2 % 2, late % 2)
-        finish_re(TILES - 1)
+
+        last = TILES - 1
+        modulate(last, 1, (1,))
+        quantize_uv(TILES, 0, 1)
+        quantize_uv(TILES, 1, 1)
+        finish_re(last - 2)
+        mix_uwa(last, 0)
+        mix_vwb(last, 0)
+        product("im", last, 0, [(0, 1)], True, False)
+        mix_uwa(last, 1)
+        finish_re(last - 1)
+        empty_uwa(last)
+        mix_vwb(last, 1)
+        product("im", last, 0, [(1, 0)], False, False)
+        mix_im(last, 1)
+        finish_re(last)
+        finish_im(last)

from contextlib import ExitStack

import concourse.mybir as mybir
from concourse.masks import make_identity

E, R, K, N = 1024, 512, 1024, 512
FLOPS = 2 * E * R * K + 4 * 2 * E * K * N

F32 = mybir.dt.float32
BF16 = mybir.dt.bfloat16
U32 = mybir.dt.uint32
U8 = mybir.dt.uint8
FP8 = mybir.dt.float8_e4m3fn
FP8X4 = mybir.dt.float8_e4m3fn_x4
ALU = mybir.AluOpType
ACT = mybir.ActivationFunctionType

P = 128
PACK = 4
K_PASS = P * PACK
G = K // K_PASS
TILES = E // P
PAIRS = TILES // 2
RUN = 4
BANKS = 8
UV_BUFS = 3
ON_GPSIMD = (3, 4)
UWA_BUFS = 3
SPLIT_FROM = 4
HALVES = 16
HALF0 = 5


def tile_escnso2radialconvolution_kernel(tc, edge, wr_bytes, wr_scale, br, x, wa, wb, out):
    nc = tc.nc
    edge_v = edge.rearrange("(p i) r -> p i r", i=TILES)
    x_v = x.rearrange("s (p i) k -> p i s k", i=TILES)
    out_v = out.rearrange("s (p i) n -> p i s n", i=TILES)
    wr_v = wr_bytes.rearrange("(p j) c -> p j c", j=PACK)
    w_v = [w.rearrange("(g p j) n -> g p j n", p=P, j=PACK) for w in (wa, wb)]

    with ExitStack() as ctx:
        sb = ctx.enter_context(tc.tile_pool(name="sb", bufs=1))
        ps = ctx.enter_context(tc.psum_pool(name="ps", bufs=1))
        ctx.enter_context(tc.manual_schedule())

        def tiles(name, count, shape, dtype):
            return [sb.tile(shape, dtype, name="%s%d" % (name, n), align_bytes=64) for n in range(count)]

        ident = sb.tile([P, P], F32, name="ident")
        warm = sb.tile([P, 8], F32, name="warm")
        scale = sb.tile([P, PACK], F32, name="scale")
        bias_bf = sb.tile([P, G, PACK], BF16, name="bias_bf")
        wr_raw = tiles("wr_raw", 2, [P, 2, K], U8)
        wr_wide = tiles("wr_wide", G, [P, PACK, K_PASS], BF16)
        wr_grp = tiles("wr_grp", G, [P, K_PASS * PACK], BF16)
        wr_codes = tiles("wr_codes", G, [P, K_PASS], U32)
        wr_scales = tiles("wr_scales", G, [P, K_PASS], U8)
        edge_raw = tiles("edge_raw", PAIRS, [P, 2, R], BF16)
        edge_grp = tiles("edge_grp", PAIRS // 2, [P, 4 * P * PACK], BF16)
        edge_codes = tiles("edge_codes", PAIRS // 2, [P, 4 * P], U32)
        edge_scales = tiles("edge_scales", PAIRS // 2, [P, 4 * P], U8)
        x_raw = tiles("x_raw", TILES, [P, 2, K], BF16)
        x_split = tiles("x_split", 2, [P, 2 * G, 2, P], F32)
        radial = tiles("radial", PAIRS * G, [P, 2, P * PACK], F32)
        w_raw = tiles("w_raw", 2 * G, [P, PACK, N], BF16)
        w_grp = tiles("w_grp", 2 * G, [P, N * PACK], BF16)
        w_grp[1] = w_grp[0]
        w_codes = tiles("w_codes", 2 * G, [P, N], U32)
        w_scales = tiles("w_scales", 2 * G, [P, N], U8)
        uv_grp = tiles("uv_grp", UV_BUFS, [P, 4 * P * PACK], BF16)
        uv_codes = tiles("uv_codes", TILES + 1, [P, 4 * P], U32)
        uv_scales = tiles("uv_scales", TILES + 1, [P, 4 * P], U8)
        u_wa = tiles("u_wa", UWA_BUFS, [P, N], F32)
        v_wb = tiles("v_wb", 2, [P, N], F32)
        res_re = tiles("res_re", TILES, [P, N], F32)
        res_im = tiles("res_im", 4, [P, N], F32)

        banks = [ps.tile([P, N], F32, name="bank%d" % n) for n in range(BANKS)]
        free = list(range(BANKS))
        held = {}

        def take_bank(key):
            held[key] = free[0]
            free.remove(held[key])
            return banks[held[key]]

        def last_read(key):
            free.append(held[key])
            return banks[held[key]]

        def quantize(codes, scales, grouped, first, count):
            nc.vector.quantize_mx(out=codes[:, first:first + count].bitcast(FP8X4), scales=scales[:, first:first + count],
                                  in_=grouped[:, PACK * first:PACK * (first + count)])

        def widen(g, j, on_vector):
            src = wr_raw[j // 2][:, j % 2, g * K_PASS:(g + 1) * K_PASS].bitcast(FP8)
            if on_vector:
                nc.vector.tensor_scalar(out=wr_wide[g][:, j, :], in0=src, scalar1=scale[:, j:j + 1], scalar2=None, op0=ALU.mult)
            else:
                nc.scalar.activation(out=wr_wide[g][:, j, :], in_=src, func=ACT.Copy, scale=scale[:, j:j + 1])

        def group_wr(g, on_vector):
            dst = wr_grp[g][:].rearrange("p (t m j) -> p m t j", t=PACK, j=PACK)
            src = wr_wide[g][:].rearrange("p j (m t) -> p m t j", t=PACK)
            if on_vector:
                nc.vector.tensor_copy(out=dst, in_=src)
            else:
                nc.scalar.copy(out=dst, in_=src)

        def group_w(w, g, on_vector):
            dst = w_grp[2 * g + w][:].rearrange("p (c q j) -> p c j q", q=RUN, j=PACK)
            src = w_raw[2 * g + w][:].rearrange("p j (c q) -> p c j q", q=RUN)
            if on_vector:
                nc.vector.tensor_copy(out=dst, in_=src)
            else:
                nc.scalar.copy(out=dst, in_=src)

        def group_w_gpsimd(w, g):
            nc.gpsimd.tensor_scalar(
                out=w_grp[2 * g + w][:].rearrange("p (n j) -> p n j", j=PACK), in0=w_raw[2 * g + w][:].rearrange("p j n -> p n j"),
                scalar1=1.0, scalar2=0.0, op0=ALU.mult, op1=ALU.add)

        def quantize_w(w, g):
            quantize(w_codes[2 * g + w], w_scales[2 * g + w], w_grp[2 * g + w], 0, N)

        def turn_edge(pair):
            bank = take_bank(("edge", pair))[:].rearrange("p (i h e) -> p i h e", i=2, h=2)
            for i in range(2):
                words = edge_raw[pair][:, i, :].bitcast(F32)
                for h in range(2):
                    nc.tensor.transpose(bank[:, i, h, :], words[:, h::2], ident[:])

        def empty_edge(pair):
            nc.scalar.copy(
                out=edge_grp[pair // 2][:, pair % 2 * 2 * K_PASS:(pair % 2 + 1) * 2 * K_PASS].bitcast(F32).rearrange("p (i e h) -> p i e h", i=2, h=2),
                in_=last_read(("edge", pair))[:].rearrange("p (i h e) -> p i e h", i=2, h=2))

        def radial_passes(pair, g, half):
            bank = take_bank(("radial", pair, g, half))
            edges = slice(pair % 2 * 2 * P, (pair % 2 + 1) * 2 * P)
            for n in range(2):
                cols = slice((2 * half + n) * P, (2 * half + n + 1) * P)
                nc.tensor.matmul_mx(
                    out=bank[:, n * 2 * P:(n + 1) * 2 * P],
                    lhsT=wr_codes[g][:, cols].bitcast(FP8X4), lhsT_scale=wr_scales[g][:, cols],
                    rhs=edge_codes[pair // 2][:, edges].bitcast(FP8X4), rhs_scale=edge_scales[pair // 2][:, edges],
                    start=True, stop=True)

        def empty_radial(pair, g, half):
            bank = last_read(("radial", pair, g, half))
            dst = radial[G * pair + g][:].rearrange("p i (c t q) -> p t i c q", t=PACK, q=RUN)
            for n in range(2):
                t = 2 * half + n
                nc.scalar.activation(
                    out=dst[:, t], in_=bank[:, n * 2 * P:(n + 1) * 2 * P].rearrange("p (i c q) -> p i c q", i=2, q=RUN),
                    func=ACT.Identity, bias=bias_bf[:, g, t:t + 1])

        def turn_x(i, g):
            bank = take_bank(("x", i, g))[:].rearrange("p (s c h q) -> p s h c q", s=2, h=2, q=RUN)
            for s in range(2):
                words = x_raw[i][:, s, g * K_PASS:(g + 1) * K_PASS].bitcast(F32)
                for h in range(2):
                    if i >= SPLIT_FROM:
                        nc.tensor.transpose(bank[:, s, h], x_split[i % 2][:, s * G + g, h, :], ident[:])
                    else:
                        nc.tensor.transpose(bank[:, s, h], words[:, h::2], ident[:])

        def split_x(i):
            words = x_raw[i][:].rearrange("p s k -> p (s k)").bitcast(F32)
            nc.scalar.copy(out=x_split[i % 2][:], in_=words.rearrange("p (a w h) -> p a h w", h=2, w=P))

        def modulate(i, g, parts=(0, 1)):
            count = len(parts)
            bank = last_read(("x", i, g)) if parts[-1] == 1 else banks[held[("x", i, g)]]
            turned = bank[:].bitcast(BF16).rearrange("p (s c h q j) -> p s c h j q", s=2, h=2, q=RUN, j=2)
            r = radial[G * (i // 2) + g][:, i % 2, :].rearrange("p (c h j q) -> p c h j q", h=2, j=2, q=RUN)
            dst = uv_grp[(i + g) % UV_BUFS][:].rearrange("p (a s c q h j) -> p a s c h j q", a=2, s=2, q=RUN, h=2, j=2)
            nc.vector.tensor_tensor(
                out=dst[:, 1 - g, parts[0]:parts[0] + count], in0=turned[:, parts[0]:parts[0] + count],
                in1=r.unsqueeze(1).to_broadcast([P, count, P // RUN, 2, 2, RUN]), op=ALU.mult)

        def quantize_uv(n, first, count):
            quantize(uv_codes[n], uv_scales[n], uv_grp[n % UV_BUFS], first * P, count * P)

        def product(name, i, g, terms, start, stop):
            acc = banks[held[(name, i)]] if (name, i) in held else take_bank((name, i))
            for n, (s, w) in enumerate(terms):
                cols = slice((2 * (1 - g) + s) * P, (2 * (1 - g) + s + 1) * P)
                nc.tensor.matmul_mx(
                    out=acc[:], lhsT=uv_codes[i + g][:, cols].bitcast(FP8X4), lhsT_scale=uv_scales[i + g][:, cols],
                    rhs=w_codes[2 * g + w][:].bitcast(FP8X4), rhs_scale=w_scales[2 * g + w][:],
                    start=(start and n == 0), stop=(stop and n == len(terms) - 1))

        def mix_uwa(i, g):
            product("uwa", i, g, [(0, 0)], g == 0, g == 1)

        def mix_vwb(i, g):
            product("vwb", i, g, [(1, 1)], g == 0, g == 1)

        def mix_im(i, g):
            product("im", i, g, [(0, 1), (1, 0)], g == 0, g == 1)

        def empty_uwa(i):
            nc.scalar.copy(out=u_wa[i % UWA_BUFS][:], in_=last_read(("uwa", i))[:])

        def finish_re(i):
            nc.vector.tensor_tensor(out=res_re[i][:], in0=u_wa[i % UWA_BUFS][:], in1=last_read(("vwb", i))[:], op=ALU.subtract)
            nc.sync.dma_start(out=out_v[:, i, 0, :], in_=res_re[i][:])

        def empty_vwb(i):
            nc.scalar.copy(out=v_wb[i % 2][:], in_=last_read(("vwb", i))[:])

        def finish_re_gpsimd(i):
            res = uv_grp[(i + 2) % UV_BUFS][:, 2 * K_PASS:].bitcast(F32)
            nc.gpsimd.tensor_tensor(out=res, in0=u_wa[i % UWA_BUFS][:], in1=v_wb[i % 2][:], op=ALU.subtract)
            nc.sync.dma_start(out=out_v[:, i, 0, :], in_=res)

        def finish_im(i):
            nc.scalar.copy(out=res_im[i % 4][:], in_=last_read(("im", i))[:])
            nc.sync.dma_start(out=out_v[:, i, 1, :], in_=res_im[i % 4][:])

        def radial_half(pair, g, half):
            radial_passes(pair, g, half)
            empty_radial(pair, g, half)

        def quantize_edge(pair, pairs):
            quantize(edge_codes[pair // 2], edge_scales[pair // 2], edge_grp[pair // 2], pair % 2 * 2 * P, pairs * 2 * P)

        def quantize_wr(g):
            quantize(wr_codes[g], wr_scales[g], wr_grp[g], 0, K_PASS)

        def load_edge(pair):
            nc.sync.dma_start(out=edge_raw[pair][:], in_=edge_v[:, 2 * pair:2 * pair + 2, :])

        def load_x(i):
            nc.sync.dma_start(out=x_raw[i][:], in_=x_v[:, i])

        def load_w(w, g):
            nc.sync.dma_start(out=w_raw[2 * g + w][:], in_=w_v[w][g])

        nc.scalar.dma_start(out=scale[:], in_=wr_scale.rearrange("(p j) o -> p (j o)", j=PACK))
        nc.sync.dma_start(out=wr_raw[0][:], in_=wr_v[:, 0:2, :])
        nc.sync.dma_start(out=wr_raw[1][:], in_=wr_v[:, 2:4, :])
        load_edge(0)
        nc.scalar.dma_start(out=bias_bf[:], in_=br.rearrange("(g p t) -> p g t", p=P, t=PACK))
        load_w(0, 0)
        load_x(0)
        load_edge(1)
        load_w(1, 0)
        load_x(1)
        load_w(0, 1)
        load_edge(2)
        load_w(1, 1)
        load_x(2)
        load_edge(3)
        for i in range(3, TILES):
            load_x(i)

        nc.vector.memset(warm[:], 0.0)
        nc.scalar.activation(out=warm[:], in_=warm[:], func=ACT.Identity)
        make_identity(nc, ident[:])

        for j in range(PACK):
            widen(0, j, True)
        for j in range(PACK):
            widen(1, j, j == 0)
        turn_edge(0)
        empty_edge(0)
        group_wr(0, True)
        group_wr(1, False)
        quantize_edge(0, 1)
        quantize_wr(0)
        turn_x(0, 0)
        radial_passes(0, 0, 0)
        radial_passes(0, 0, 1)
        turn_edge(1)
        empty_radial(0, 0, 0)
        empty_radial(0, 0, 1)
        empty_edge(1)
        turn_x(0, 1)
        group_w(0, 0, True)
        quantize_wr(1)
        quantize_w(0, 0)
        group_w_gpsimd(1, 0)
        radial_half(0, 1, 0)
        radial_half(0, 1, 1)
        turn_x(1, 0)
        turn_x(1, 1)
        group_w(0, 1, False)
        group_w(1, 1, False)
        modulate(0, 0)
        turn_edge(2)
        modulate(1, 0)
        turn_x(2, 0)
        modulate(0, 1)
        turn_x(2, 1)
        quantize_edge(1, 1)
        quantize_uv(0, 2, 2)
        quantize_w(1, 0)
        radial_passes(1, 0, 0)
        radial_passes(1, 0, 1)
        quantize_w(0, 1)
        quantize_uv(1, 0, 4)
        mix_im(0, 0)
        mix_uwa(0, 0)
        modulate(1, 1)
        empty_edge(2)
        empty_radial(1, 0, 0)
        empty_radial(1, 0, 1)
        mix_uwa(0, 1)
        quantize_w(1, 1)
        quantize_edge(2, 1)
        radial_half(1, 1, 0)
        radial_half(1, 1, 1)
        mix_im(0, 1)
        mix_vwb(0, 0)
        mix_vwb(0, 1)
        radial_passes(2, 0, 0)
        empty_uwa(0)
        turn_edge(3)
        finish_im(0)
        empty_radial(2, 0, 0)
        empty_edge(3)

        for i in range(2, TILES):
            m = i - 1
            early, late = 2 * i + HALF0, 2 * i + HALF0 + 1
            modulate(i, 0)
            quantize_uv(i, 0, 2)
            if i == 3:
                quantize_edge(3, 1)
            quantize_uv(i, 2, 2)
            mix_vwb(m, 0)
            mix_im(m, 0)
            mix_uwa(m, 0)
            if SPLIT_FROM <= i + 2 < TILES:
                split_x(i + 2)
            if i + 1 < TILES:
                turn_x(i + 1, 0)
                turn_x(i + 1, 1)
            if early < HALVES:
                radial_passes(early // 4, early // 2 % 2, early % 2)
            modulate(i, 1, (0, 1) if i + 1 < TILES else (0,))
            if early < HALVES:
                empty_radial(early // 4, early // 2 % 2, early % 2)
            if m in ON_GPSIMD:
                mix_uwa(m, 1)
                mix_vwb(m, 1)
                mix_im(m, 1)
            else:
                mix_im(m, 1)
                mix_uwa(m, 1)
                mix_vwb(m, 1)
            if m - 1 in ON_GPSIMD:
                finish_re_gpsimd(m - 1)
            elif i + 1 < TILES:
                finish_re(m - 1)
            if m in ON_GPSIMD:
                empty_uwa(m)
                empty_vwb(m)
                finish_im(m)
            else:
                finish_im(m)
                empty_uwa(m)
            if late < HALVES:
                radial_half(late // 4, late // 2 % 2, late % 2)

        last = TILES - 1
        modulate(last, 1, (1,))
        quantize_uv(TILES, 0, 1)
        quantize_uv(TILES, 1, 1)
        finish_re(last - 2)
        mix_uwa(last, 0)
        mix_vwb(last, 0)
        product("im", last, 0, [(0, 1)], True, False)
        mix_uwa(last, 1)
        finish_re(last - 1)
        empty_uwa(last)
        mix_vwb(last, 1)
        product("im", last, 0, [(1, 0)], False, False)
        mix_im(last, 1)
        finish_re(last)
        finish_im(last)
